import numpy as np
import ml_dtypes


def mxq(x, axis, fmt="e4m3"):
    dtype, down = {"e4m3": (ml_dtypes.float8_e4m3fn, 7), "e5m2": (ml_dtypes.float8_e5m2, 14)}[fmt]
    v = np.moveaxis(np.asarray(x, np.float32).astype(ml_dtypes.bfloat16).astype(np.float64), axis, -1)
    blocks = v.reshape(v.shape[:-1] + (-1, 32))
    amax = np.abs(blocks).max(-1, keepdims=True)
    byte = np.maximum(np.where(amax > 0, np.frexp(amax)[1] - 1 + 127, 0) - down, 1)
    scale = np.exp2(byte - 127.0)
    codes = (blocks / scale).astype(np.float32).astype(dtype).astype(np.float64)
    return np.moveaxis((codes * scale).reshape(v.shape), -1, axis)


WIDE = False


def mx_kscale(k):
    if not WIDE:
        return np.ones(k)
    levels = np.array([10, -10, 5, -5, 0])
    if k % 512:
        return np.exp2(np.random.permutation(np.resize(levels, k // 32))).repeat(32)
    a = np.empty((k // 512, 16))
    for p in range(k // 512):
        a[p, :8] = np.random.permutation(np.resize(levels, 8))
        for g in range(8):
            far = levels[np.abs(levels - a[p, g]) >= 10]
            a[p, g + 8] = far[np.random.randint(len(far))]
    return np.exp2(a.ravel()).repeat(32)


def f64(x):
    return np.asarray(x).astype(np.float64)


def striped(idx):
    return np.tile(idx.reshape(-1, 16).T, (8, 1)).astype(np.uint16)


def unstriped(offs):
    return offs[:16].T.reshape(-1).astype(np.int64)


def striped8(idx):
    return np.concatenate([x.reshape(-1, 16).T for x in idx]).astype(np.uint16)


def runs(offs, k):
    lists = np.stack([offs[16 * r : 16 * r + 16].T.reshape(-1) for r in range(8)]).astype(np.int64)
    return lists[np.arange(k) % 512 // 64]


def pack_weight(w):
    k, n = w.shape
    w = f64(np.asarray(w, np.float32).astype(ml_dtypes.bfloat16)).reshape(k // 32, 32, n)
    amax = np.abs(w).max(1)
    byte = np.clip(np.where(amax > 0, np.frexp(amax)[1] - 1 + 127 - 7, 1), 1, 254)
    scaled = (w * np.exp2(127.0 - byte)[:, None, :]).reshape(k, n).astype(np.float32)
    words = np.ascontiguousarray(scaled.reshape(k // 512, 128, 4, n).transpose(0, 1, 3, 2)).astype(ml_dtypes.float8_e4m3fn).view(np.uint8)
    return words, np.ascontiguousarray(byte.astype(np.uint8).reshape(k // 512, 16, n))


def unpack_weight(words, scales):
    g, p, n, _ = words.shape
    vals = np.ascontiguousarray(words).view(ml_dtypes.float8_e4m3fn).astype(np.float64) * np.repeat(np.exp2(scales.astype(np.float64) - 127.0), 8, axis=1)[..., None]
    return vals.transpose(0, 1, 3, 2).reshape(g * 512, n)


def sigmoid(v):
    return 1.0 / (1.0 + np.exp(-np.maximum(v, -700.0)))

def planes(y):
    n, m = y.shape
    v = y.astype(np.float32).astype(ml_dtypes.bfloat16).astype(np.float64).reshape(n // 32, 32, m)
    top = np.abs(v).max(1)
    byte = np.clip(np.where(top > 0, np.frexp(top)[1] - 1 + 127 - 7, 1), 1, 254)
    codes = (v * np.exp2(127.0 - byte)[:, None, :]).reshape(n, m).astype(np.float32).astype(ml_dtypes.float8_e4m3fn).view(np.uint8)
    words = codes.reshape(n // 512, 128, 4, m).transpose(0, 1, 3, 2)
    return np.ascontiguousarray(words), np.ascontiguousarray(byte.astype(np.uint8).reshape(n // 512, 16, m))


K, T, S, N, H = 512, 2048, 512, 512, 512


def setup_inputs():
    n = np.random.standard_normal
    s = mx_kscale(K)[:, None]
    u = mx_kscale(H)
    packed_xT = pack_weight(n((K, T)) * s)
    packed_w1 = pack_weight(n((K, H)) / np.sqrt(K) / s)
    packed_w2 = pack_weight(n((K, H)) / np.sqrt(K) / s)
    packed_w3 = pack_weight(n((H, N)) / np.sqrt(2 * H) / u[:, None])
    packed_w4 = pack_weight(n((H, N)) / np.sqrt(2 * H) / u[:, None])
    return {
        "x_words": packed_xT[0],
        "x_scales": packed_xT[1],
        "w1_words": packed_w1[0],
        "w1_scales": packed_w1[1],
        "w2_words": packed_w2[0],
        "w2_scales": packed_w2[1],
        "gn": (np.random.uniform(0.5, 1.5, (H, 1)) * u[:, None]).astype(np.float32),
        "gm": (np.random.uniform(0.5, 1.5, (H, 1)) * u[:, None]).astype(np.float32),
        "w3_words": packed_w3[0],
        "w3_scales": packed_w3[1],
        "w4_words": packed_w4[0],
        "w4_scales": packed_w4[1],
        "offs": striped(np.random.permutation(T)[:S]),
        "hz": striped8(np.random.randint(0, T, (8, S))),
        "n1": striped8(np.stack([np.random.permutation(S) for _ in range(8)])),
        "n2": striped8(np.stack([np.random.permutation(S) for _ in range(8)])),
        "n3": striped8(np.stack([np.random.permutation(S) for _ in range(8)])),
        "n4": striped8(np.stack([np.random.permutation(S) for _ in range(8)])),
        "n5": striped8(np.stack([np.random.permutation(S) for _ in range(8)])),
        "n6": striped8(np.stack([np.random.permutation(S) for _ in range(8)])),
        "n7": striped8(np.stack([np.random.permutation(S) for _ in range(8)])),
        "n8": striped8(np.stack([np.random.permutation(S) for _ in range(8)])),
    }


def reference(x_words, x_scales, w1_words, w1_scales, w2_words, w2_scales, gn, gm, w3_words, w3_scales, w4_words, w4_scales, offs, hz, n1, n2, n3, n4, n5, n6, n7, n8):
    xq = unpack_weight(x_words, x_scales)[:, unstriped(offs)]
    y = unpack_weight(w1_words, w1_scales).T @ xq
    b1 = y[np.arange(H)[:, None], runs(n1, H)]
    b2 = y[np.arange(H)[:, None], runs(n2, H)]
    b3 = y[np.arange(H)[:, None], runs(n3, H)]
    z = f64(gn) * (np.maximum(np.maximum(b1, b2), b3) - (0.5 * (np.maximum(np.minimum(b1, b2), np.minimum(np.maximum(b1, b2), b3)))))
    x_hz = unpack_weight(x_words, x_scales)[np.arange(K)[:, None], runs(hz, K)]
    d = unpack_weight(w2_words, w2_scales).T @ x_hz
    z2 = f64(gm) * ((d * (d[np.arange(H)[:, None], runs(n4, H)])) * (np.tanh(d[np.arange(H)[:, None], runs(n5, H)])))
    h = unpack_weight(w3_words, w3_scales).T @ mxq(z, 0, "e4m3") + unpack_weight(w4_words, w4_scales).T @ mxq(z2, 0, "e4m3")
    out_0 = (h[np.arange(N)[:, None], runs(n6, N)]) * sigmoid(h) + (h[np.arange(N)[:, None], runs(n7, N)]) * (sigmoid(h[np.arange(N)[:, None], runs(n8, N)]))
    return (out_0,) + planes(out_0)

@@ -1,0 +1,314 @@
+from contextlib import ExitStack
+
+import concourse.mybir as mybir
+
+F32 = mybir.dt.float32
+BF16 = mybir.dt.bfloat16
+I32 = mybir.dt.int32
+U32 = mybir.dt.uint32
+U16 = mybir.dt.uint16
+U8 = mybir.dt.uint8
+FP8X4 = mybir.dt.float8_e4m3fn_x4
+ALU = mybir.AluOpType
+ACT = mybir.ActivationFunctionType
+
+P = 128
+T = 2048
+S = 512
+PACK = 4
+FLOPS = 4 * 2 * 512 * 512 * 512
+
+MID_CHUNKS = (256, 256)
+OUT_CHUNKS = (256, 128, 128)
+N4_PLANES_ON_SCALAR = 4
+
+
+def spans(widths):
+    result, start = [], 0
+    for width in widths:
+        result.append((start, width))
+        start = start + width
+    return result
+
+
+def woven(ap):
+    return ap.rearrange("p (c i t) -> p c t i", i=2, t=PACK)
+
+
+def planes_by_pairs(ap):
+    return ap.rearrange("p t (c i) -> p c t i", i=2)
+
+
+def tile_picked_hjointop2cubewsum_none_po_kernel(
+    tc, x_words, x_scales, w1_words, w1_scales, w2_words, w2_scales, gn, gm,
+    w3_words, w3_scales, w4_words, w4_scales, offs, hz, n1, n2, n3, n4, n5, n6, n7, n8,
+    out_0, out_1, out_2,
+):
+    nc = tc.nc
+    with ExitStack() as ctx:
+        lists = ctx.enter_context(tc.tile_pool(name="lists", bufs=1))
+        sb = ctx.enter_context(tc.tile_pool(name="sb", bufs=1))
+        psum = ctx.enter_context(tc.psum_pool(name="psum", bufs=1))
+
+        def load_list(name, source):
+            tile = lists.tile([P, S // 16], U16, name=name)
+            nc.sync.dma_start(tile[:], source)
+            return tile
+
+        def load_words(name, source, width):
+            tile = sb.tile([P, width], U32, name=name, align_bytes=64)
+            nc.sync.dma_start(tile[:].bitcast(I32), source[0].rearrange("p n t -> p (n t)").bitcast(I32))
+            return tile
+
+        def cleared_bytes(name, width):
+            tile = sb.tile([P, width], U8, name=name, align_bytes=64)
+            nc.vector.memset(tile[:].bitcast(I32), 0)
+            return tile
+
+        def load_scale_row(queue, tile, first, source, r):
+            rows = source[0].rearrange("(q r) n -> r q n", r=4)
+            queue.dma_start(tile[first:P:32, :].bitcast(I32), rows[r].bitcast(I32))
+
+        def dealt_words(name, raw):
+            tile = sb.tile([P, S], U32, name=name, align_bytes=64)
+            nc.vector.tensor_copy(
+                tile[:].bitcast(I32).rearrange("p (t c i) -> p c t i", t=PACK, i=4),
+                raw[:].bitcast(I32).rearrange("p (c i t) -> p c t i", t=PACK, i=4),
+            )
+            return tile
+
+        def dealt_bytes(name, raw):
+            tile = sb.tile([P, S], U8, name=name, align_bytes=64)
+            nc.vector.tensor_copy(
+                tile[:].rearrange("p (t m) -> p t m", t=PACK),
+                raw[:].rearrange("p (m t) -> p t m", t=PACK),
+            )
+            return tile
+
+        def cut(offsets, start, width):
+            return offsets[:, start // 16 : (start + width) // 16]
+
+        xs = cleared_bytes("xs", T)
+        s1 = cleared_bytes("s1", S)
+        xs_runs = cleared_bytes("xs_runs", T)
+        s234 = cleared_bytes("s234", S)
+        hs = cleared_bytes("hs", S)
+        w1r = load_words("w1r", w1_words, S)
+        for r in range(4):
+            load_scale_row(nc.sync, xs, r, x_scales, r)
+        offs_l = load_list("offs_l", offs)
+        gn_t = sb.tile([P, PACK], F32, name="gn_t")
+        nc.sync.dma_start(gn_t[:], gn.rearrange("(p t) o -> p (t o)", t=PACK))
+        xw = load_words("xw", x_words, T)
+        for r in range(4):
+            load_scale_row(nc.sync, s1, r, w1_scales, r)
+        hz_l = load_list("hz_l", hz)
+        n1_l = load_list("n1_l", n1)
+        n3_l = load_list("n3_l", n3)
+        n2_l = load_list("n2_l", n2)
+        for r in range(4):
+            load_scale_row(nc.sync, xs_runs, r if r < 2 else 14 + r, x_scales, r)
+        w2r = load_words("w2r", w2_words, S)
+        w3r = load_words("w3r", w3_words, S)
+        w4r = load_words("w4r", w4_words, S)
+        for a, source in enumerate((w2_scales, w3_scales, w4_scales)):
+            for r in range(4):
+                load_scale_row(nc.sync, s234, 4 * a + r, source, r)
+        gm_t = sb.tile([P, PACK], F32, name="gm_t")
+        nc.sync.dma_start(gm_t[:], gm.rearrange("(p t) o -> p (t o)", t=PACK))
+        n5_l = load_list("n5_l", n5)
+        n4_l = load_list("n4_l", n4)
+        n7_l = load_list("n7_l", n7)
+        n6_l = load_list("n6_l", n6)
+        n8_l = load_list("n8_l", n8)
+
+        y_win = [sb.tile([P, 2 * S], F32, name="y_win%d" % t) for t in range(PACK)]
+        for t in range(PACK):
+            nc.gpsimd.memset(y_win[t][:, S : 2 * S], 0.0)
+
+        tok_bytes = sb.tile([P, S], U8, name="tok_bytes", align_bytes=64)
+        nc.vector.tensor_copy(tok_bytes[:], xs[:].indirect(offs_l[:]))
+        tok_words = sb.tile([P, S], U32, name="tok_words", align_bytes=64)
+        nc.vector.tensor_copy(tok_words[:], xw[:].indirect(offs_l[:]))
+        w1d = dealt_words("w1d", w1r)
+        s1d = dealt_bytes("s1d", s1)
+
+        step = sb.tile([P, PACK], F32, name="step")
+        nc.gpsimd.tensor_scalar(step[:], gn_t[:], 0.0, 2.0, ALU.is_ge, ALU.mult)
+        sign = sb.tile([P, PACK], F32, name="sign")
+        nc.gpsimd.tensor_scalar(sign[:], step[:], 1.0, -1.0, ALU.mult, ALU.add)
+        half_sign = sb.tile([P, PACK], F32, name="half_sign")
+        nc.gpsimd.tensor_scalar(half_sign[:], step[:], 0.5, -0.5, ALU.mult, ALU.add)
+        half_gain = sb.tile([P, PACK], F32, name="half_gain")
+        nc.gpsimd.tensor_tensor(half_gain[:], gn_t[:], half_sign[:], ALU.mult)
+        signs = sb.tile([P, PACK], BF16, name="signs")
+        nc.gpsimd.tensor_copy(signs[:], sign[:])
+
+        hz_words = sb.tile([P, S], U32, name="hz_words", align_bytes=64)
+        nc.vector.tensor_copy(hz_words[:], xw[:].indirect(hz_l[:]))
+        hz_bytes = sb.tile([P, S], U8, name="hz_bytes", align_bytes=64)
+        nc.vector.tensor_copy(hz_bytes[:], xs_runs[:].indirect(hz_l[:]))
+        for r in range(4):
+            first = r if r < 2 else 14 + r
+            nc.sync.dma_start(hs[r:P:32, :].bitcast(I32), hz_bytes[first:P:32, :].bitcast(I32))
+
+        for t in range(PACK):
+            cols = slice(t * P, (t + 1) * P)
+            bank = psum.tile([P, S], F32, name="y_bank%d" % t, tag="bank%d" % t)
+            nc.tensor.matmul_mx(
+                out=bank[:], lhsT=w1d[:, cols].bitcast(FP8X4), lhsT_scale=s1d[:, cols],
+                rhs=tok_words[:].bitcast(FP8X4), rhs_scale=tok_bytes[:], start=True, stop=True,
+            )
+            win = y_win[t]
+            if t == 0:
+                nc.scalar.activation(win[:, 0:S], bank[:], ACT.Copy, scale=half_gain[:, t : t + 1])
+            else:
+                nc.vector.tensor_scalar(win[:, 0:S], bank[:], half_gain[:, t : t + 1], None, ALU.mult)
+
+        mid_spans = spans(MID_CHUNKS)
+
+        def planes(name, width):
+            return sb.tile([P, PACK, width], F32, name=name)
+
+        def quantised(name, values, width):
+            words = sb.tile([P, width], U32, name=name + "_words", align_bytes=64)
+            scales = sb.tile([P, width], U8, name=name + "_bytes", align_bytes=64)
+            nc.vector.quantize_mx(out=words[:].bitcast(FP8X4), scales=scales[:], in_=values[:])
+            return words, scales
+
+        b1, b2, c3 = planes("b1", S), planes("b2", S), planes("c3", S)
+        hi2, lo, mid, top2, med = planes("hi2", S), planes("lo", S), planes("mid", S), planes("top2", S), planes("med", S)
+
+        def rank_three(t):
+            nc.scalar.activation(b1[:, t, :], y_win[t][:].indirect(n1_l[:]), ACT.Copy)
+            nc.scalar.activation(c3[:, t, :], y_win[t][:].indirect(n3_l[:]), ACT.Copy, scale=2.0)
+            nc.scalar.activation(b2[:, t, :], y_win[t][:].indirect(n2_l[:]), ACT.Copy)
+            nc.vector.scalar_tensor_tensor(hi2[:, t, :], b1[:, t, :], 2.0, c3[:, t, :], ALU.mult, ALU.max)
+            nc.vector.scalar_tensor_tensor(lo[:, t, :], c3[:, t, :], 0.5, b1[:, t, :], ALU.mult, ALU.min)
+            nc.vector.scalar_tensor_tensor(mid[:, t, :], hi2[:, t, :], 0.5, b2[:, t, :], ALU.mult, ALU.min)
+            nc.vector.scalar_tensor_tensor(top2[:, t, :], b2[:, t, :], 2.0, hi2[:, t, :], ALU.mult, ALU.max)
+            nc.vector.tensor_tensor(med[:, t, :], lo[:, t, :], mid[:, t, :], ALU.max)
+
+        rank_three(0)
+        w2d = dealt_words("w2d", w2r)
+        s234d = dealt_bytes("s234d", s234)
+        d_banks = []
+        for t in range(PACK):
+            cols = slice(t * P, (t + 1) * P)
+            bank = psum.tile([P, S], F32, name="d_bank%d" % t, tag="bank%d" % (PACK + t))
+            nc.tensor.matmul_mx(
+                out=bank[:], lhsT=w2d[:, cols].bitcast(FP8X4), lhsT_scale=s234d[:, cols],
+                rhs=hz_words[:].bitcast(FP8X4), rhs_scale=hs[:], start=True, stop=True,
+            )
+            d_banks.append(bank)
+        d_win = [sb.tile([P, S], F32, name="d_win%d" % t) for t in range(PACK)]
+        th_win = [sb.tile([P, S], F32, name="th_win%d" % t) for t in range(PACK)]
+        w3d = dealt_words("w3d", w3r)
+        w4d = dealt_words("w4d", w4r)
+        rank_three(1)
+        for t in (0, 1):
+            nc.vector.tensor_copy(d_win[t][:], d_banks[t][:])
+        rank_three(2)
+        for t in (2, 3):
+            nc.vector.tensor_copy(d_win[t][:], d_banks[t][:])
+        rank_three(3)
+        for t in range(PACK):
+            nc.scalar.activation(th_win[t][:], d_banks[t][:], ACT.Tanh)
+
+        z_abs = sb.tile([P, PACK * S], BF16, name="z_abs", align_bytes=64)
+        z = sb.tile([P, PACK * S], BF16, name="z", align_bytes=64)
+        for start, width in mid_spans:
+            places = slice(start, start + width)
+            nc.vector.tensor_tensor(woven(z_abs[:, PACK * start : PACK * (start + width)]),
+                                    planes_by_pairs(top2[:, :, places]), planes_by_pairs(med[:, :, places]), ALU.subtract)
+        for start, width in mid_spans:
+            cols = slice(PACK * start, PACK * (start + width))
+            nc.vector.tensor_tensor(
+                z[:, cols].rearrange("p (c t) -> p c t", t=PACK), z_abs[:, cols].rearrange("p (c t) -> p c t", t=PACK),
+                signs[:].unsqueeze(1).to_broadcast([P, width, PACK]), ALU.mult)
+        z_words, z_bytes = quantised("z", z, S)
+
+        h_win = [sb.tile([P, S], F32, name="h_win%d" % t) for t in range(PACK)]
+        sg_win = [sb.tile([P, S], F32, name="sg_win%d" % t) for t in range(PACK)]
+        h_banks = {}
+
+        def neighbours_of_d(c):
+            start, width = mid_spans[c]
+            th, d4, prod = planes("th_%d" % c, width), planes("d4_%d" % c, width), planes("prod_%d" % c, width)
+            for t in range(PACK):
+                nc.scalar.activation(th[:, t, :], th_win[t][:].indirect(cut(n5_l, start, width)), ACT.Copy)
+                window = d_win[t][:].indirect(cut(n4_l, start, width))
+                if c == len(mid_spans) - 1 and t >= PACK - N4_PLANES_ON_SCALAR:
+                    nc.scalar.activation(d4[:, t, :], window, ACT.Copy)
+                    nc.vector.tensor_tensor(prod[:, t, :], d4[:, t, :], th[:, t, :], ALU.mult)
+                else:
+                    nc.vector.tensor_tensor(prod[:, t, :], window, th[:, t, :], ALU.mult)
+            rows = sb.tile([P, PACK, width], BF16, name="z2_rows%d" % c)
+            for t in range(PACK):
+                nc.vector.scalar_tensor_tensor(rows[:, t, :], prod[:, t, :], gm_t[:, t : t + 1],
+                                               d_win[t][:, start : start + width], ALU.mult, ALU.mult)
+            return rows
+
+        def make_h(c, rows):
+            start, width = mid_spans[c]
+            places = slice(start, start + width)
+            z2 = sb.tile([P, PACK * width], BF16, name="z2_%d" % c, align_bytes=64)
+            nc.vector.tensor_copy(woven(z2[:]), planes_by_pairs(rows[:]))
+            z2_words, z2_bytes = quantised("z2_%d" % c, z2, width)
+            for t in range(PACK):
+                cols = slice(t * P, (t + 1) * P)
+                bank = psum.tile([P, width], F32, name="h_bank%d_%d" % (c, t), tag="bank%d" % (PACK * c + t))
+                nc.tensor.matmul_mx(
+                    out=bank[:], lhsT=w3d[:, cols].bitcast(FP8X4), lhsT_scale=s234d[4:P, cols],
+                    rhs=z_words[:, places].bitcast(FP8X4), rhs_scale=z_bytes[:, places], start=True, stop=False,
+                )
+                nc.tensor.matmul_mx(
+                    out=bank[:], lhsT=w4d[:, cols].bitcast(FP8X4), lhsT_scale=s234d[8:P, cols],
+                    rhs=z2_words[:].bitcast(FP8X4), rhs_scale=z2_bytes[:], start=False, stop=True,
+                )
+                h_banks[(c, t)] = bank
+
+        def empty_h(c):
+            start, width = mid_spans[c]
+            places = slice(start, start + width)
+            for t in range(PACK):
+                nc.scalar.activation(h_win[t][:, places], h_banks[(c, t)][:], ACT.Copy)
+            for t in range(PACK):
+                nc.scalar.activation(sg_win[t][:, places], h_banks[(c, t)][:], ACT.Sigmoid)
+
+        make_h(0, neighbours_of_d(0))
+        make_h(1, neighbours_of_d(1))
+        empty_h(0)
+        empty_h(1)
+
+        out_rows = out_0.rearrange("(p t) j -> p t j", t=PACK)
+        out_words = out_1[0].rearrange("p n t -> p (n t)").bitcast(I32)
+        o_words = sb.tile([P, S], U32, name="o_words", align_bytes=64)
+        o_bytes = sb.tile([P, S], U8, name="o_bytes", align_bytes=64)
+        out_spans = spans(OUT_CHUNKS)
+        first = planes("first", S)
+        for start, width in mid_spans:
+            places = slice(start, start + width)
+            for t in range(PACK):
+                nc.vector.tensor_tensor(first[:, t, places], h_win[t][:].indirect(cut(n6_l, start, width)), sg_win[t][:, places], ALU.mult)
+        for c, (start, width) in enumerate(out_spans):
+            places = slice(start, start + width)
+            last = c == len(out_spans) - 1
+            h7 = planes("h7_%d" % c, width)
+            second = planes("second%d" % c, width)
+            for t in range(PACK):
+                nc.scalar.activation(h7[:, t, :], h_win[t][:].indirect(cut(n7_l, start, width)), ACT.Copy)
+                window = sg_win[t][:].indirect(cut(n8_l, start, width))
+                nc.vector.tensor_tensor(second[:, t, :], window, h7[:, t, :], ALU.mult)
+            result = planes("result%d" % c, width)
+            nc.vector.tensor_tensor(result[:], first[:, :, places], second[:], ALU.add)
+            nc.sync.dma_start(out_rows[:, :, places], result[:])
+            rounded = sb.tile([P, PACK * width], BF16, name="rounded%d" % c, align_bytes=64)
+            if last:
+                nc.vector.tensor_copy(woven(rounded[:]), planes_by_pairs(result[:]))
+            else:
+                nc.scalar.copy(woven(rounded[:]), planes_by_pairs(result[:]))
+            nc.vector.quantize_mx(out=o_words[:, places].bitcast(FP8X4), scales=o_bytes[:, places], in_=rounded[:])
+            nc.sync.dma_start(out_words[:, places], o_words[:, places].bitcast(I32))
+        for q in range(4):
+            nc.scalar.dma_start(out_2[0, 4 * q : 4 * q + 4, :].bitcast(I32), o_bytes[32 * q : 32 * q + 4, :].bitcast(I32))

@@ -21,6 +21,7 @@ FLOPS = 4 * 2 * 512 * 512 * 512
 MID_CHUNKS = (256, 256)
 OUT_CHUNKS = (256, 128, 128)
 N4_PLANES_ON_SCALAR = 4
+D_COPIES_ON_VECTOR = 2
 
 
 def spans(widths):
@@ -91,7 +92,8 @@ def tile_picked_hjointop2cubewsum_none_po_kernel(
         xs = cleared_bytes("xs", T)
         s1 = cleared_bytes("s1", S)
         xs_runs = cleared_bytes("xs_runs", T)
-        s234 = cleared_bytes("s234", S)
+        s2 = cleared_bytes("s2", S)
+        s34 = cleared_bytes("s34", S)
         hs = cleared_bytes("hs", S)
         w1r = load_words("w1r", w1_words, S)
         for r in range(4):
@@ -109,22 +111,15 @@ def tile_picked_hjointop2cubewsum_none_po_kernel(
         for r in range(4):
             load_scale_row(nc.sync, xs_runs, r if r < 2 else 14 + r, x_scales, r)
         w2r = load_words("w2r", w2_words, S)
-        w3r = load_words("w3r", w3_words, S)
-        w4r = load_words("w4r", w4_words, S)
-        for a, source in enumerate((w2_scales, w3_scales, w4_scales)):
-            for r in range(4):
-                load_scale_row(nc.sync, s234, 4 * a + r, source, r)
-        gm_t = sb.tile([P, PACK], F32, name="gm_t")
-        nc.sync.dma_start(gm_t[:], gm.rearrange("(p t) o -> p (t o)", t=PACK))
-        n5_l = load_list("n5_l", n5)
-        n4_l = load_list("n4_l", n4)
-        n7_l = load_list("n7_l", n7)
-        n6_l = load_list("n6_l", n6)
-        n8_l = load_list("n8_l", n8)
+        for r in range(4):
+            load_scale_row(nc.sync, s2, r, w2_scales, r)
 
         y_win = [sb.tile([P, 2 * S], F32, name="y_win%d" % t) for t in range(PACK)]
         for t in range(PACK):
-            nc.gpsimd.memset(y_win[t][:, S : 2 * S], 0.0)
+            nc.vector.memset(y_win[t][:, S : 2 * S], 0.0)
+
+        warm = sb.tile([P, 1], F32, name="warm")
+        nc.scalar.activation(warm[:], y_win[0][:, S : S + 1], ACT.Sigmoid)
 
         tok_bytes = sb.tile([P, S], U8, name="tok_bytes", align_bytes=64)
         nc.vector.tensor_copy(tok_bytes[:], xs[:].indirect(offs_l[:]))
@@ -151,6 +146,19 @@ def tile_picked_hjointop2cubewsum_none_po_kernel(
         for r in range(4):
             first = r if r < 2 else 14 + r
             nc.sync.dma_start(hs[r:P:32, :].bitcast(I32), hz_bytes[first:P:32, :].bitcast(I32))
+        gm_t = sb.tile([P, PACK], F32, name="gm_t")
+        nc.sync.dma_start(gm_t[:], gm.rearrange("(p t) o -> p (t o)", t=PACK))
+        n5_l = load_list("n5_l", n5)
+        n4_l = load_list("n4_l", n4)
+        w3r = load_words("w3r", w3_words, S)
+        w4r = load_words("w4r", w4_words, S)
+        for a, source in enumerate((w3_scales, w4_scales)):
+            for r in range(4):
+                load_scale_row(nc.sync, s34, 4 * a + r, source, r)
+        n7_l = load_list("n7_l", n7)
+        n6_l = load_list("n6_l", n6)
+        n8_l = load_list("n8_l", n8)
+
 
         for t in range(PACK):
             cols = slice(t * P, (t + 1) * P)
@@ -167,8 +175,8 @@ def tile_picked_hjointop2cubewsum_none_po_kernel(
 
         mid_spans = spans(MID_CHUNKS)
 
-        def planes(name, width):
-            return sb.tile([P, PACK, width], F32, name=name)
+        def planes(name, width, tag=None):
+            return sb.tile([P, PACK, width], F32, name=name, tag=tag or name)
 
         def quantised(name, values, width):
             words = sb.tile([P, width], U32, name=name + "_words", align_bytes=64)
@@ -179,93 +187,113 @@ def tile_picked_hjointop2cubewsum_none_po_kernel(
         b1, b2, c3 = planes("b1", S), planes("b2", S), planes("c3", S)
         hi2, lo, mid, top2, med = planes("hi2", S), planes("lo", S), planes("mid", S), planes("top2", S), planes("med", S)
 
-        def rank_three(t):
-            nc.scalar.activation(b1[:, t, :], y_win[t][:].indirect(n1_l[:]), ACT.Copy)
-            nc.scalar.activation(c3[:, t, :], y_win[t][:].indirect(n3_l[:]), ACT.Copy, scale=2.0)
-            nc.scalar.activation(b2[:, t, :], y_win[t][:].indirect(n2_l[:]), ACT.Copy)
-            nc.vector.scalar_tensor_tensor(hi2[:, t, :], b1[:, t, :], 2.0, c3[:, t, :], ALU.mult, ALU.max)
-            nc.vector.scalar_tensor_tensor(lo[:, t, :], c3[:, t, :], 0.5, b1[:, t, :], ALU.mult, ALU.min)
-            nc.vector.scalar_tensor_tensor(mid[:, t, :], hi2[:, t, :], 0.5, b2[:, t, :], ALU.mult, ALU.min)
-            nc.vector.scalar_tensor_tensor(top2[:, t, :], b2[:, t, :], 2.0, hi2[:, t, :], ALU.mult, ALU.max)
-            nc.vector.tensor_tensor(med[:, t, :], lo[:, t, :], mid[:, t, :], ALU.max)
+        def rank_three(t0, t1):
+            for t in range(t0, t1):
+                nc.scalar.activation(b1[:, t, :], y_win[t][:].indirect(n1_l[:]), ACT.Copy)
+                nc.scalar.activation(c3[:, t, :], y_win[t][:].indirect(n3_l[:]), ACT.Copy, scale=2.0)
+            for t in range(t0, t1):
+                nc.scalar.activation(b2[:, t, :], y_win[t][:].indirect(n2_l[:]), ACT.Copy)
+            ts = slice(t0, t1)
+            nc.vector.scalar_tensor_tensor(hi2[:, ts, :], b1[:, ts, :], 2.0, c3[:, ts, :], ALU.mult, ALU.max)
+            nc.vector.scalar_tensor_tensor(lo[:, ts, :], c3[:, ts, :], 0.5, b1[:, ts, :], ALU.mult, ALU.min)
+            nc.vector.scalar_tensor_tensor(mid[:, ts, :], hi2[:, ts, :], 0.5, b2[:, ts, :], ALU.mult, ALU.min)
+            nc.vector.scalar_tensor_tensor(top2[:, ts, :], b2[:, ts, :], 2.0, hi2[:, ts, :], ALU.mult, ALU.max)
+            nc.vector.tensor_tensor(med[:, ts, :], lo[:, ts, :], mid[:, ts, :], ALU.max)
 
-        rank_three(0)
         w2d = dealt_words("w2d", w2r)
-        s234d = dealt_bytes("s234d", s234)
+        s2d = dealt_bytes("s2d", s2)
+        rank_three(0, 1)
         d_banks = []
         for t in range(PACK):
             cols = slice(t * P, (t + 1) * P)
             bank = psum.tile([P, S], F32, name="d_bank%d" % t, tag="bank%d" % (PACK + t))
             nc.tensor.matmul_mx(
-                out=bank[:], lhsT=w2d[:, cols].bitcast(FP8X4), lhsT_scale=s234d[:, cols],
+                out=bank[:], lhsT=w2d[:, cols].bitcast(FP8X4), lhsT_scale=s2d[:, cols],
                 rhs=hz_words[:].bitcast(FP8X4), rhs_scale=hs[:], start=True, stop=True,
             )
             d_banks.append(bank)
         d_win = [sb.tile([P, S], F32, name="d_win%d" % t) for t in range(PACK)]
         th_win = [sb.tile([P, S], F32, name="th_win%d" % t) for t in range(PACK)]
+        for t in range(D_COPIES_ON_VECTOR):
+            nc.vector.tensor_copy(d_win[t][:], d_banks[t][:])
         w3d = dealt_words("w3d", w3r)
         w4d = dealt_words("w4d", w4r)
-        rank_three(1)
-        for t in (0, 1):
-            nc.vector.tensor_copy(d_win[t][:], d_banks[t][:])
-        rank_three(2)
-        for t in (2, 3):
-            nc.vector.tensor_copy(d_win[t][:], d_banks[t][:])
-        rank_three(3)
-        for t in range(PACK):
-            nc.scalar.activation(th_win[t][:], d_banks[t][:], ACT.Tanh)
+        s34d = dealt_bytes("s34d", s34)
+        rank_three(1, 2)
+        rank_three(2, 3)
+        rank_three(3, 4)
 
         z_abs = sb.tile([P, PACK * S], BF16, name="z_abs", align_bytes=64)
         z = sb.tile([P, PACK * S], BF16, name="z", align_bytes=64)
-        for start, width in mid_spans:
+        z_words = sb.tile([P, S], U32, name="z_words", align_bytes=64)
+        z_bytes = sb.tile([P, S], U8, name="z_bytes", align_bytes=64)
+
+        def z_unsigned(c):
+            start, width = mid_spans[c]
             places = slice(start, start + width)
             nc.vector.tensor_tensor(woven(z_abs[:, PACK * start : PACK * (start + width)]),
                                     planes_by_pairs(top2[:, :, places]), planes_by_pairs(med[:, :, places]), ALU.subtract)
-        for start, width in mid_spans:
+
+        def z_signed(c):
+            start, width = mid_spans[c]
             cols = slice(PACK * start, PACK * (start + width))
             nc.vector.tensor_tensor(
                 z[:, cols].rearrange("p (c t) -> p c t", t=PACK), z_abs[:, cols].rearrange("p (c t) -> p c t", t=PACK),
                 signs[:].unsqueeze(1).to_broadcast([P, width, PACK]), ALU.mult)
-        z_words, z_bytes = quantised("z", z, S)
+
+        def z_quantised(c):
+            start, width = mid_spans[c]
+            places = slice(start, start + width)
+            nc.vector.quantize_mx(out=z_words[:, places].bitcast(FP8X4), scales=z_bytes[:, places],
+                                  in_=z[:, PACK * start : PACK * (start + width)])
 
         h_win = [sb.tile([P, S], F32, name="h_win%d" % t) for t in range(PACK)]
         sg_win = [sb.tile([P, S], F32, name="sg_win%d" % t) for t in range(PACK)]
         h_banks = {}
 
-        def neighbours_of_d(c):
-            start, width = mid_spans[c]
-            th, d4, prod = planes("th_%d" % c, width), planes("d4_%d" % c, width), planes("prod_%d" % c, width)
-            for t in range(PACK):
-                nc.scalar.activation(th[:, t, :], th_win[t][:].indirect(cut(n5_l, start, width)), ACT.Copy)
-                window = d_win[t][:].indirect(cut(n4_l, start, width))
-                if c == len(mid_spans) - 1 and t >= PACK - N4_PLANES_ON_SCALAR:
-                    nc.scalar.activation(d4[:, t, :], window, ACT.Copy)
-                    nc.vector.tensor_tensor(prod[:, t, :], d4[:, t, :], th[:, t, :], ALU.mult)
-                else:
-                    nc.vector.tensor_tensor(prod[:, t, :], window, th[:, t, :], ALU.mult)
-            rows = sb.tile([P, PACK, width], BF16, name="z2_rows%d" % c)
-            for t in range(PACK):
-                nc.vector.scalar_tensor_tensor(rows[:, t, :], prod[:, t, :], gm_t[:, t : t + 1],
-                                               d_win[t][:, start : start + width], ALU.mult, ALU.mult)
-            return rows
+        th = [planes("th_%d" % c, width) for c, (start, width) in enumerate(mid_spans)]
+        prod = [planes("prod_%d" % c, width) for c, (start, width) in enumerate(mid_spans)]
+        z2_rows = [sb.tile([P, PACK, width], BF16, name="z2_rows%d" % c) for c, (start, width) in enumerate(mid_spans)]
+        d4 = planes("d4", mid_spans[-1][1])
 
-        def make_h(c, rows):
+        def neighbour_product(c, t):
+            start, width = mid_spans[c]
+            nc.scalar.activation(th[c][:, t, :], th_win[t][:].indirect(cut(n5_l, start, width)), ACT.Copy)
+            window = d_win[t][:].indirect(cut(n4_l, start, width))
+            if c == len(mid_spans) - 1 and t >= PACK - N4_PLANES_ON_SCALAR:
+                nc.scalar.activation(d4[:, t, :], window, ACT.Copy)
+                nc.vector.tensor_tensor(prod[c][:, t, :], d4[:, t, :], th[c][:, t, :], ALU.mult)
+            else:
+                nc.vector.tensor_tensor(prod[c][:, t, :], window, th[c][:, t, :], ALU.mult)
+
+        def z2_row(c, t):
+            start, width = mid_spans[c]
+            nc.vector.scalar_tensor_tensor(z2_rows[c][:, t, :], prod[c][:, t, :], gm_t[:, t : t + 1],
+                                           d_win[t][:, start : start + width], ALU.mult, ALU.mult)
+
+        z2 = [sb.tile([P, PACK * width], BF16, name="z2_%d" % c, align_bytes=64) for c, (start, width) in enumerate(mid_spans)]
+
+        def z2_woven(c):
+            nc.vector.tensor_copy(woven(z2[c][:]), planes_by_pairs(z2_rows[c][:]))
+
+        def make_h(c):
             start, width = mid_spans[c]
             places = slice(start, start + width)
-            z2 = sb.tile([P, PACK * width], BF16, name="z2_%d" % c, align_bytes=64)
-            nc.vector.tensor_copy(woven(z2[:]), planes_by_pairs(rows[:]))
-            z2_words, z2_bytes = quantised("z2_%d" % c, z2, width)
+            z2_words, z2_bytes = quantised("z2_%d" % c, z2[c], width)
             for t in range(PACK):
                 cols = slice(t * P, (t + 1) * P)
                 bank = psum.tile([P, width], F32, name="h_bank%d_%d" % (c, t), tag="bank%d" % (PACK * c + t))
-                nc.tensor.matmul_mx(
-                    out=bank[:], lhsT=w3d[:, cols].bitcast(FP8X4), lhsT_scale=s234d[4:P, cols],
-                    rhs=z_words[:, places].bitcast(FP8X4), rhs_scale=z_bytes[:, places], start=True, stop=False,
-                )
-                nc.tensor.matmul_mx(
-                    out=bank[:], lhsT=w4d[:, cols].bitcast(FP8X4), lhsT_scale=s234d[8:P, cols],
-                    rhs=z2_words[:].bitcast(FP8X4), rhs_scale=z2_bytes[:], start=False, stop=True,
-                )
+                passes = [
+                    (w4d[:, cols], s34d[4:P, cols], z2_words[:], z2_bytes[:]),
+                    (w3d[:, cols], s34d[:, cols], z_words[:, places], z_bytes[:, places]),
+                ]
+                if c == 1:
+                    passes = passes[::-1]
+                for k, (w, w_scale, values, values_scale) in enumerate(passes):
+                    nc.tensor.matmul_mx(
+                        out=bank[:], lhsT=w.bitcast(FP8X4), lhsT_scale=w_scale,
+                        rhs=values.bitcast(FP8X4), rhs_scale=values_scale, start=(k == 0), stop=(k == 1),
+                    )
                 h_banks[(c, t)] = bank
 
         def empty_h(c):
@@ -276,8 +304,25 @@ def tile_picked_hjointop2cubewsum_none_po_kernel(
             for t in range(PACK):
                 nc.scalar.activation(sg_win[t][:, places], h_banks[(c, t)][:], ACT.Sigmoid)
 
-        make_h(0, neighbours_of_d(0))
-        make_h(1, neighbours_of_d(1))
+        z_steps = [(z_unsigned, 0), (z_signed, 0), (z_unsigned, 1), (z_signed, 1)]
+        for t in range(PACK):
+            nc.scalar.activation(th_win[t][:], d_banks[t][:], ACT.Tanh)
+            if t >= D_COPIES_ON_VECTOR:
+                nc.scalar.activation(d_win[t][:], d_banks[t][:], ACT.Copy)
+            neighbour_product(0, t)
+            z_steps[t][0](z_steps[t][1])
+            z2_row(0, t)
+        z_quantised(0)
+        z2_woven(0)
+        z_quantised(1)
+        make_h(0)
+        for t in range(PACK):
+            neighbour_product(1, t)
+            if t > 0:
+                z2_row(1, t - 1)
+        z2_row(1, PACK - 1)
+        z2_woven(1)
+        make_h(1)
         empty_h(0)
         empty_h(1)
 
@@ -291,23 +336,34 @@ def tile_picked_hjointop2cubewsum_none_po_kernel(
             places = slice(start, start + width)
             for t in range(PACK):
                 nc.vector.tensor_tensor(first[:, t, places], h_win[t][:].indirect(cut(n6_l, start, width)), sg_win[t][:, places], ALU.mult)
+        last = len(out_spans) - 1
+        h7 = planes("h7", S)
+        g8 = planes("g8", out_spans[last][1])
+        for c, (start, width) in enumerate(out_spans):
+            for t in range(PACK):
+                nc.scalar.activation(h7[:, t, start : start + width], h_win[t][:].indirect(cut(n7_l, start, width)), ACT.Copy)
+                if c == last:
+                    nc.scalar.activation(g8[:, t, :], sg_win[t][:].indirect(cut(n8_l, start, width)), ACT.Copy)
+        results = []
         for c, (start, width) in enumerate(out_spans):
             places = slice(start, start + width)
-            last = c == len(out_spans) - 1
-            h7 = planes("h7_%d" % c, width)
             second = planes("second%d" % c, width)
-            for t in range(PACK):
-                nc.scalar.activation(h7[:, t, :], h_win[t][:].indirect(cut(n7_l, start, width)), ACT.Copy)
-                window = sg_win[t][:].indirect(cut(n8_l, start, width))
-                nc.vector.tensor_tensor(second[:, t, :], window, h7[:, t, :], ALU.mult)
+            if c == last:
+                nc.vector.tensor_tensor(second[:], g8[:], h7[:, :, places], ALU.mult)
+            else:
+                for t in range(PACK):
+                    nc.vector.tensor_tensor(second[:, t, :], sg_win[t][:].indirect(cut(n8_l, start, width)), h7[:, t, places], ALU.mult)
             result = planes("result%d" % c, width)
             nc.vector.tensor_tensor(result[:], first[:, :, places], second[:], ALU.add)
             nc.sync.dma_start(out_rows[:, :, places], result[:])
+            results.append(result)
+        for c, (start, width) in enumerate(out_spans):
+            places = slice(start, start + width)
             rounded = sb.tile([P, PACK * width], BF16, name="rounded%d" % c, align_bytes=64)
-            if last:
-                nc.vector.tensor_copy(woven(rounded[:]), planes_by_pairs(result[:]))
+            if c == last:
+                nc.vector.tensor_copy(woven(rounded[:]), planes_by_pairs(results[c][:]))
             else:
-                nc.scalar.copy(woven(rounded[:]), planes_by_pairs(result[:]))
+                nc.scalar.copy(woven(rounded[:]), planes_by_pairs(results[c][:]))
             nc.vector.quantize_mx(out=o_words[:, places].bitcast(FP8X4), scales=o_bytes[:, places], in_=rounded[:])
             nc.sync.dma_start(out_words[:, places], o_words[:, places].bitcast(I32))
         for q in range(4):

@@ -129,15 +129,11 @@ def tile_picked_hjointop2cubewsum_none_po_kernel(
         s1d = dealt_bytes("s1d", s1)
 
         step = sb.tile([P, PACK], F32, name="step")
-        nc.gpsimd.tensor_scalar(step[:], gn_t[:], 0.0, 2.0, ALU.is_ge, ALU.mult)
-        sign = sb.tile([P, PACK], F32, name="sign")
-        nc.gpsimd.tensor_scalar(sign[:], step[:], 1.0, -1.0, ALU.mult, ALU.add)
-        half_sign = sb.tile([P, PACK], F32, name="half_sign")
-        nc.gpsimd.tensor_scalar(half_sign[:], step[:], 0.5, -0.5, ALU.mult, ALU.add)
+        nc.vector.tensor_scalar(step[:], gn_t[:], 0.0, -0.5, ALU.is_ge, ALU.add)
         half_gain = sb.tile([P, PACK], F32, name="half_gain")
-        nc.gpsimd.tensor_tensor(half_gain[:], gn_t[:], half_sign[:], ALU.mult)
+        nc.vector.tensor_tensor(half_gain[:], gn_t[:], step[:], ALU.mult)
         signs = sb.tile([P, PACK], BF16, name="signs")
-        nc.gpsimd.tensor_copy(signs[:], sign[:])
+        nc.vector.tensor_scalar(signs[:], step[:], 2.0, None, ALU.mult)
 
         hz_words = sb.tile([P, S], U32, name="hz_words", align_bytes=64)
         nc.vector.tensor_copy(hz_words[:], xw[:].indirect(hz_l[:]))

from contextlib import ExitStack

import concourse.mybir as mybir

F32 = mybir.dt.float32
BF16 = mybir.dt.bfloat16
I32 = mybir.dt.int32
U32 = mybir.dt.uint32
U16 = mybir.dt.uint16
U8 = mybir.dt.uint8
FP8X4 = mybir.dt.float8_e4m3fn_x4
ALU = mybir.AluOpType
ACT = mybir.ActivationFunctionType

P = 128
T = 2048
S = 512
PACK = 4
FLOPS = 4 * 2 * 512 * 512 * 512

MID_CHUNKS = (256, 256)
OUT_CHUNKS = (256, 128, 128)
N4_PLANES_ON_SCALAR = 4
D_COPIES_ON_VECTOR = 2


def spans(widths):
    result, start = [], 0
    for width in widths:
        result.append((start, width))
        start = start + width
    return result


def woven(ap):
    return ap.rearrange("p (c i t) -> p c t i", i=2, t=PACK)


def planes_by_pairs(ap):
    return ap.rearrange("p t (c i) -> p c t i", i=2)


def tile_picked_hjointop2cubewsum_none_po_kernel(
    tc, x_words, x_scales, w1_words, w1_scales, w2_words, w2_scales, gn, gm,
    w3_words, w3_scales, w4_words, w4_scales, offs, hz, n1, n2, n3, n4, n5, n6, n7, n8,
    out_0, out_1, out_2,
):
    nc = tc.nc
    with ExitStack() as ctx:
        lists = ctx.enter_context(tc.tile_pool(name="lists", bufs=1))
        sb = ctx.enter_context(tc.tile_pool(name="sb", bufs=1))
        psum = ctx.enter_context(tc.psum_pool(name="psum", bufs=1))

        def load_list(name, source):
            tile = lists.tile([P, S // 16], U16, name=name)
            nc.sync.dma_start(tile[:], source)
            return tile

        def load_words(name, source, width):
            tile = sb.tile([P, width], U32, name=name, align_bytes=64)
            nc.sync.dma_start(tile[:].bitcast(I32), source[0].rearrange("p n t -> p (n t)").bitcast(I32))
            return tile

        def cleared_bytes(name, width):
            tile = sb.tile([P, width], U8, name=name, align_bytes=64)
            nc.vector.memset(tile[:].bitcast(I32), 0)
            return tile

        def load_scale_row(queue, tile, first, source, r):
            rows = source[0].rearrange("(q r) n -> r q n", r=4)
            queue.dma_start(tile[first:P:32, :].bitcast(I32), rows[r].bitcast(I32))

        def dealt_words(name, raw):
            tile = sb.tile([P, S], U32, name=name, align_bytes=64)
            nc.vector.tensor_copy(
                tile[:].bitcast(I32).rearrange("p (t c i) -> p c t i", t=PACK, i=4),
                raw[:].bitcast(I32).rearrange("p (c i t) -> p c t i", t=PACK, i=4),
            )
            return tile

        def dealt_bytes(name, raw):
            tile = sb.tile([P, S], U8, name=name, align_bytes=64)
            nc.vector.tensor_copy(
                tile[:].rearrange("p (t m) -> p t m", t=PACK),
                raw[:].rearrange("p (m t) -> p t m", t=PACK),
            )
            return tile

        def cut(offsets, start, width):
            return offsets[:, start // 16 : (start + width) // 16]

        xs = cleared_bytes("xs", T)
        s1 = cleared_bytes("s1", S)
        xs_runs = cleared_bytes("xs_runs", T)
        s2 = cleared_bytes("s2", S)
        s34 = cleared_bytes("s34", S)
        hs = cleared_bytes("hs", S)
        w1r = load_words("w1r", w1_words, S)
        for r in range(4):
            load_scale_row(nc.sync, xs, r, x_scales, r)
        offs_l = load_list("offs_l", offs)
        gn_t = sb.tile([P, PACK], F32, name="gn_t")
        nc.sync.dma_start(gn_t[:], gn.rearrange("(p t) o -> p (t o)", t=PACK))
        xw = load_words("xw", x_words, T)
        for r in range(4):
            load_scale_row(nc.sync, s1, r, w1_scales, r)
        hz_l = load_list("hz_l", hz)
        n1_l = load_list("n1_l", n1)
        n3_l = load_list("n3_l", n3)
        n2_l = load_list("n2_l", n2)
        for r in range(4):
            load_scale_row(nc.sync, xs_runs, r if r < 2 else 14 + r, x_scales, r)
        w2r = load_words("w2r", w2_words, S)
        for r in range(4):
            load_scale_row(nc.sync, s2, r, w2_scales, r)

        y_win = [sb.tile([P, 2 * S], F32, name="y_win%d" % t) for t in range(PACK)]
        for t in range(PACK):
            nc.vector.memset(y_win[t][:, S : 2 * S], 0.0)

        warm = sb.tile([P, 1], F32, name="warm")
        nc.scalar.activation(warm[:], y_win[0][:, S : S + 1], ACT.Sigmoid)

        tok_bytes = sb.tile([P, S], U8, name="tok_bytes", align_bytes=64)
        nc.vector.tensor_copy(tok_bytes[:], xs[:].indirect(offs_l[:]))
        tok_words = sb.tile([P, S], U32, name="tok_words", align_bytes=64)
        nc.vector.tensor_copy(tok_words[:], xw[:].indirect(offs_l[:]))
        w1d = dealt_words("w1d", w1r)
        s1d = dealt_bytes("s1d", s1)

        step = sb.tile([P, PACK], F32, name="step")
        nc.vector.tensor_scalar(step[:], gn_t[:], 0.0, -0.5, ALU.is_ge, ALU.add)
        half_gain = sb.tile([P, PACK], F32, name="half_gain")
        nc.vector.tensor_tensor(half_gain[:], gn_t[:], step[:], ALU.mult)
        signs = sb.tile([P, PACK], BF16, name="signs")
        nc.vector.tensor_scalar(signs[:], step[:], 2.0, None, ALU.mult)

        hz_words = sb.tile([P, S], U32, name="hz_words", align_bytes=64)
        nc.vector.tensor_copy(hz_words[:], xw[:].indirect(hz_l[:]))
        hz_bytes = sb.tile([P, S], U8, name="hz_bytes", align_bytes=64)
        nc.vector.tensor_copy(hz_bytes[:], xs_runs[:].indirect(hz_l[:]))
        for r in range(4):
            first = r if r < 2 else 14 + r
            nc.sync.dma_start(hs[r:P:32, :].bitcast(I32), hz_bytes[first:P:32, :].bitcast(I32))
        gm_t = sb.tile([P, PACK], F32, name="gm_t")
        nc.sync.dma_start(gm_t[:], gm.rearrange("(p t) o -> p (t o)", t=PACK))
        n5_l = load_list("n5_l", n5)
        n4_l = load_list("n4_l", n4)
        w3r = load_words("w3r", w3_words, S)
        w4r = load_words("w4r", w4_words, S)
        for a, source in enumerate((w3_scales, w4_scales)):
            for r in range(4):
                load_scale_row(nc.sync, s34, 4 * a + r, source, r)
        n7_l = load_list("n7_l", n7)
        n6_l = load_list("n6_l", n6)
        n8_l = load_list("n8_l", n8)


        for t in range(PACK):
            cols = slice(t * P, (t + 1) * P)
            bank = psum.tile([P, S], F32, name="y_bank%d" % t, tag="bank%d" % t)
            nc.tensor.matmul_mx(
                out=bank[:], lhsT=w1d[:, cols].bitcast(FP8X4), lhsT_scale=s1d[:, cols],
                rhs=tok_words[:].bitcast(FP8X4), rhs_scale=tok_bytes[:], start=True, stop=True,
            )
            win = y_win[t]
            if t == 0:
                nc.scalar.activation(win[:, 0:S], bank[:], ACT.Copy, scale=half_gain[:, t : t + 1])
            else:
                nc.vector.tensor_scalar(win[:, 0:S], bank[:], half_gain[:, t : t + 1], None, ALU.mult)

        mid_spans = spans(MID_CHUNKS)

        def planes(name, width, tag=None):
            return sb.tile([P, PACK, width], F32, name=name, tag=tag or name)

        def quantised(name, values, width):
            words = sb.tile([P, width], U32, name=name + "_words", align_bytes=64)
            scales = sb.tile([P, width], U8, name=name + "_bytes", align_bytes=64)
            nc.vector.quantize_mx(out=words[:].bitcast(FP8X4), scales=scales[:], in_=values[:])
            return words, scales

        b1, b2, c3 = planes("b1", S), planes("b2", S), planes("c3", S)
        hi2, lo, mid, top2, med = planes("hi2", S), planes("lo", S), planes("mid", S), planes("top2", S), planes("med", S)

        def rank_three(t0, t1):
            for t in range(t0, t1):
                nc.scalar.activation(b1[:, t, :], y_win[t][:].indirect(n1_l[:]), ACT.Copy)
                nc.scalar.activation(c3[:, t, :], y_win[t][:].indirect(n3_l[:]), ACT.Copy, scale=2.0)
            for t in range(t0, t1):
                nc.scalar.activation(b2[:, t, :], y_win[t][:].indirect(n2_l[:]), ACT.Copy)
            ts = slice(t0, t1)
            nc.vector.scalar_tensor_tensor(hi2[:, ts, :], b1[:, ts, :], 2.0, c3[:, ts, :], ALU.mult, ALU.max)
            nc.vector.scalar_tensor_tensor(lo[:, ts, :], c3[:, ts, :], 0.5, b1[:, ts, :], ALU.mult, ALU.min)
            nc.vector.scalar_tensor_tensor(mid[:, ts, :], hi2[:, ts, :], 0.5, b2[:, ts, :], ALU.mult, ALU.min)
            nc.vector.scalar_tensor_tensor(top2[:, ts, :], b2[:, ts, :], 2.0, hi2[:, ts, :], ALU.mult, ALU.max)
            nc.vector.tensor_tensor(med[:, ts, :], lo[:, ts, :], mid[:, ts, :], ALU.max)

        w2d = dealt_words("w2d", w2r)
        s2d = dealt_bytes("s2d", s2)
        rank_three(0, 1)
        d_banks = []
        for t in range(PACK):
            cols = slice(t * P, (t + 1) * P)
            bank = psum.tile([P, S], F32, name="d_bank%d" % t, tag="bank%d" % (PACK + t))
            nc.tensor.matmul_mx(
                out=bank[:], lhsT=w2d[:, cols].bitcast(FP8X4), lhsT_scale=s2d[:, cols],
                rhs=hz_words[:].bitcast(FP8X4), rhs_scale=hs[:], start=True, stop=True,
            )
            d_banks.append(bank)
        d_win = [sb.tile([P, S], F32, name="d_win%d" % t) for t in range(PACK)]
        th_win = [sb.tile([P, S], F32, name="th_win%d" % t) for t in range(PACK)]
        for t in range(D_COPIES_ON_VECTOR):
            nc.vector.tensor_copy(d_win[t][:], d_banks[t][:])
        w3d = dealt_words("w3d", w3r)
        w4d = dealt_words("w4d", w4r)
        s34d = dealt_bytes("s34d", s34)
        rank_three(1, 2)
        rank_three(2, 3)
        rank_three(3, 4)

        z_abs = sb.tile([P, PACK * S], BF16, name="z_abs", align_bytes=64)
        z = sb.tile([P, PACK * S], BF16, name="z", align_bytes=64)
        z_words = sb.tile([P, S], U32, name="z_words", align_bytes=64)
        z_bytes = sb.tile([P, S], U8, name="z_bytes", align_bytes=64)

        def z_unsigned(c):
            start, width = mid_spans[c]
            places = slice(start, start + width)
            nc.vector.tensor_tensor(woven(z_abs[:, PACK * start : PACK * (start + width)]),
                                    planes_by_pairs(top2[:, :, places]), planes_by_pairs(med[:, :, places]), ALU.subtract)

        def z_signed(c):
            start, width = mid_spans[c]
            cols = slice(PACK * start, PACK * (start + width))
            nc.vector.tensor_tensor(
                z[:, cols].rearrange("p (c t) -> p c t", t=PACK), z_abs[:, cols].rearrange("p (c t) -> p c t", t=PACK),
                signs[:].unsqueeze(1).to_broadcast([P, width, PACK]), ALU.mult)

        def z_quantised(c):
            start, width = mid_spans[c]
            places = slice(start, start + width)
            nc.vector.quantize_mx(out=z_words[:, places].bitcast(FP8X4), scales=z_bytes[:, places],
                                  in_=z[:, PACK * start : PACK * (start + width)])

        h_win = [sb.tile([P, S], F32, name="h_win%d" % t) for t in range(PACK)]
        sg_win = [sb.tile([P, S], F32, name="sg_win%d" % t) for t in range(PACK)]
        h_banks = {}

        th = [planes("th_%d" % c, width) for c, (start, width) in enumerate(mid_spans)]
        prod = [planes("prod_%d" % c, width) for c, (start, width) in enumerate(mid_spans)]
        z2_rows = [sb.tile([P, PACK, width], BF16, name="z2_rows%d" % c) for c, (start, width) in enumerate(mid_spans)]
        d4 = planes("d4", mid_spans[-1][1])

        def neighbour_product(c, t):
            start, width = mid_spans[c]
            nc.scalar.activation(th[c][:, t, :], th_win[t][:].indirect(cut(n5_l, start, width)), ACT.Copy)
            window = d_win[t][:].indirect(cut(n4_l, start, width))
            if c == len(mid_spans) - 1 and t >= PACK - N4_PLANES_ON_SCALAR:
                nc.scalar.activation(d4[:, t, :], window, ACT.Copy)
                nc.vector.tensor_tensor(prod[c][:, t, :], d4[:, t, :], th[c][:, t, :], ALU.mult)
            else:
                nc.vector.tensor_tensor(prod[c][:, t, :], window, th[c][:, t, :], ALU.mult)

        def z2_row(c, t):
            start, width = mid_spans[c]
            nc.vector.scalar_tensor_tensor(z2_rows[c][:, t, :], prod[c][:, t, :], gm_t[:, t : t + 1],
                                           d_win[t][:, start : start + width], ALU.mult, ALU.mult)

        z2 = [sb.tile([P, PACK * width], BF16, name="z2_%d" % c, align_bytes=64) for c, (start, width) in enumerate(mid_spans)]

        def z2_woven(c):
            nc.vector.tensor_copy(woven(z2[c][:]), planes_by_pairs(z2_rows[c][:]))

        def make_h(c):
            start, width = mid_spans[c]
            places = slice(start, start + width)
            z2_words, z2_bytes = quantised("z2_%d" % c, z2[c], width)
            for t in range(PACK):
                cols = slice(t * P, (t + 1) * P)
                bank = psum.tile([P, width], F32, name="h_bank%d_%d" % (c, t), tag="bank%d" % (PACK * c + t))
                passes = [
                    (w4d[:, cols], s34d[4:P, cols], z2_words[:], z2_bytes[:]),
                    (w3d[:, cols], s34d[:, cols], z_words[:, places], z_bytes[:, places]),
                ]
                if c == 1:
                    passes = passes[::-1]
                for k, (w, w_scale, values, values_scale) in enumerate(passes):
                    nc.tensor.matmul_mx(
                        out=bank[:], lhsT=w.bitcast(FP8X4), lhsT_scale=w_scale,
                        rhs=values.bitcast(FP8X4), rhs_scale=values_scale, start=(k == 0), stop=(k == 1),
                    )
                h_banks[(c, t)] = bank

        def empty_h(c):
            start, width = mid_spans[c]
            places = slice(start, start + width)
            for t in range(PACK):
                nc.scalar.activation(h_win[t][:, places], h_banks[(c, t)][:], ACT.Copy)
            for t in range(PACK):
                nc.scalar.activation(sg_win[t][:, places], h_banks[(c, t)][:], ACT.Sigmoid)

        z_steps = [(z_unsigned, 0), (z_signed, 0), (z_unsigned, 1), (z_signed, 1)]
        for t in range(PACK):
            nc.scalar.activation(th_win[t][:], d_banks[t][:], ACT.Tanh)
            if t >= D_COPIES_ON_VECTOR:
                nc.scalar.activation(d_win[t][:], d_banks[t][:], ACT.Copy)
            neighbour_product(0, t)
            z_steps[t][0](z_steps[t][1])
            z2_row(0, t)
        z_quantised(0)
        z2_woven(0)
        z_quantised(1)
        make_h(0)
        for t in range(PACK):
            neighbour_product(1, t)
            if t > 0:
                z2_row(1, t - 1)
        z2_row(1, PACK - 1)
        z2_woven(1)
        make_h(1)
        empty_h(0)
        empty_h(1)

        out_rows = out_0.rearrange("(p t) j -> p t j", t=PACK)
        out_words = out_1[0].rearrange("p n t -> p (n t)").bitcast(I32)
        o_words = sb.tile([P, S], U32, name="o_words", align_bytes=64)
        o_bytes = sb.tile([P, S], U8, name="o_bytes", align_bytes=64)
        out_spans = spans(OUT_CHUNKS)
        first = planes("first", S)
        for start, width in mid_spans:
            places = slice(start, start + width)
            for t in range(PACK):
                nc.vector.tensor_tensor(first[:, t, places], h_win[t][:].indirect(cut(n6_l, start, width)), sg_win[t][:, places], ALU.mult)
        last = len(out_spans) - 1
        h7 = planes("h7", S)
        g8 = planes("g8", out_spans[last][1])
        for c, (start, width) in enumerate(out_spans):
            for t in range(PACK):
                nc.scalar.activation(h7[:, t, start : start + width], h_win[t][:].indirect(cut(n7_l, start, width)), ACT.Copy)
                if c == last:
                    nc.scalar.activation(g8[:, t, :], sg_win[t][:].indirect(cut(n8_l, start, width)), ACT.Copy)
        results = []
        for c, (start, width) in enumerate(out_spans):
            places = slice(start, start + width)
            second = planes("second%d" % c, width)
            if c == last:
                nc.vector.tensor_tensor(second[:], g8[:], h7[:, :, places], ALU.mult)
            else:
                for t in range(PACK):
                    nc.vector.tensor_tensor(second[:, t, :], sg_win[t][:].indirect(cut(n8_l, start, width)), h7[:, t, places], ALU.mult)
            result = planes("result%d" % c, width)
            nc.vector.tensor_tensor(result[:], first[:, :, places], second[:], ALU.add)
            nc.sync.dma_start(out_rows[:, :, places], result[:])
            results.append(result)
        for c, (start, width) in enumerate(out_spans):
            places = slice(start, start + width)
            rounded = sb.tile([P, PACK * width], BF16, name="rounded%d" % c, align_bytes=64)
            if c == last:
                nc.vector.tensor_copy(woven(rounded[:]), planes_by_pairs(results[c][:]))
            else:
                nc.scalar.copy(woven(rounded[:]), planes_by_pairs(results[c][:]))
            nc.vector.quantize_mx(out=o_words[:, places].bitcast(FP8X4), scales=o_bytes[:, places], in_=rounded[:])
            nc.sync.dma_start(out_words[:, places], o_words[:, places].bitcast(I32))
        for q in range(4):
            nc.scalar.dma_start(out_2[0, 4 * q : 4 * q + 4, :].bitcast(I32), o_bytes[32 * q : 32 * q + 4, :].bitcast(I32))
